import numpy as np
import ml_dtypes


def mxq(x, axis, fmt="e4m3"):
    dtype, down = {"e4m3": (ml_dtypes.float8_e4m3fn, 7), "e5m2": (ml_dtypes.float8_e5m2, 14)}[fmt]
    v = np.moveaxis(np.asarray(x, np.float32).astype(ml_dtypes.bfloat16).astype(np.float64), axis, -1)
    blocks = v.reshape(v.shape[:-1] + (-1, 32))
    amax = np.abs(blocks).max(-1, keepdims=True)
    byte = np.maximum(np.where(amax > 0, np.frexp(amax)[1] - 1 + 127, 0) - down, 1)
    scale = np.exp2(byte - 127.0)
    codes = (blocks / scale).astype(np.float32).astype(dtype).astype(np.float64)
    return np.moveaxis((codes * scale).reshape(v.shape), -1, axis)


WIDE = False


def mx_kscale(k):
    if not WIDE:
        return np.ones(k)
    levels = np.array([10, -10, 5, -5, 0])
    if k % 512:
        return np.exp2(np.random.permutation(np.resize(levels, k // 32))).repeat(32)
    a = np.empty((k // 512, 16))
    for p in range(k // 512):
        a[p, :8] = np.random.permutation(np.resize(levels, 8))
        for g in range(8):
            far = levels[np.abs(levels - a[p, g]) >= 10]
            a[p, g + 8] = far[np.random.randint(len(far))]
    return np.exp2(a.ravel()).repeat(32)


def f64(x):
    return np.asarray(x).astype(np.float64)


def striped(idx):
    return np.tile(idx.reshape(-1, 16).T, (8, 1)).astype(np.uint16)


def unstriped(offs):
    return offs[:16].T.reshape(-1).astype(np.int64)


def pack_weight(w):
    k, n = w.shape
    w = f64(np.asarray(w, np.float32).astype(ml_dtypes.bfloat16)).reshape(k // 32, 32, n)
    amax = np.abs(w).max(1)
    byte = np.clip(np.where(amax > 0, np.frexp(amax)[1] - 1 + 127 - 7, 1), 1, 254)
    scaled = (w * np.exp2(127.0 - byte)[:, None, :]).reshape(k, n).astype(np.float32)
    words = np.ascontiguousarray(scaled.reshape(k // 512, 128, 4, n).transpose(0, 1, 3, 2)).astype(ml_dtypes.float8_e4m3fn).view(np.uint8)
    return words, np.ascontiguousarray(byte.astype(np.uint8).reshape(k // 512, 16, n))


def unpack_weight(words, scales):
    g, p, n, _ = words.shape
    vals = np.ascontiguousarray(words).view(ml_dtypes.float8_e4m3fn).astype(np.float64) * np.repeat(np.exp2(scales.astype(np.float64) - 127.0), 8, axis=1)[..., None]
    return vals.transpose(0, 1, 3, 2).reshape(g * 512, n)


def relu2(v):
    return np.maximum(v, 0.0) ** 2


K, T, E, C, N = 1536, 1536, 8, 256, 128
PAD = 32


def by_expert(wq, xq):
    return np.concatenate([wq[e].T @ xq[:, e * C:(e + 1) * C] for e in range(E)], axis=1)


def setup_inputs():
    n = np.random.standard_normal
    s = mx_kscale(K)[:, None]
    first = np.random.permutation(np.repeat(np.arange(E), T // E))
    second = (first + 1 + np.random.permutation(np.repeat(np.arange(E - 1), -(-T // (E - 1)))[:T])) % E
    while np.bincount(second, minlength=E).max() != T // E:
        load = np.bincount(second, minlength=E); hi, lo = int(load.argmax()), int(load.argmin())
        t = np.flatnonzero((second == hi) & (first != lo))[0]; second[t] = lo
    slot_token = np.empty(E * C, np.int64); pos = np.empty((2, T), np.int64); fill = np.zeros(E, np.int64)
    place = np.stack([np.random.permutation(C) for _ in range(E)])
    for r, deal in enumerate((first, second)):
        for t in np.random.permutation(T):
            e = deal[t]
            if fill[e] < C: j = e * C + place[e, fill[e]]; fill[e] += 1; slot_token[j] = t; pos[r, t] = j
            else: pos[r, t] = E * C + t % PAD
    g = np.random.uniform(0.2, 0.8, T)
    packed = [pack_weight(m) for m in n((E, K, N)) / np.sqrt(K) / s[None]]
    return {
        "xT": (n((K, T)) * s).astype(np.float32),
        "w_words": np.stack([m[0] for m in packed]),
        "w_scales": np.stack([m[1] for m in packed]),
        "b": (0.3 * n((N, E))).astype(np.float32),
        "gate": np.stack([np.tile(g, (N, 1)), np.tile(1.0 - g, (N, 1))]).astype(np.float32),
        "offs": striped(slot_token),
        "pos1": striped(pos[0]),
        "pos2": striped(pos[1]),
    }


def reference(xT, w_words, w_scales, b, gate, offs, pos1, pos2):
    idx = unstriped(offs)
    w = np.stack([unpack_weight(w_words[e], w_scales[e]) for e in range(E)])
    xq = mxq(f64(xT)[:, idx], 0, "e4m3")
    y = by_expert(w, xq)
    y = relu2(y + np.repeat(f64(b), C, axis=1))
    y = np.concatenate([y, np.zeros((N, PAD))], axis=1)
    return f64(gate[0]) * y[:, unstriped(pos1)] + f64(gate[1]) * y[:, unstriped(pos2)]

@@ -1,0 +1,142 @@
+from contextlib import ExitStack
+
+import concourse.mybir as mybir
+
+K, T, E, C, N = 1536, 1536, 8, 256, 128
+S = E * C
+PAD = 32
+P = 128
+PACK = 4
+K_PASS = P * PACK
+PASSES = K // K_PASS
+
+FLOPS = 2 * K * N * S
+
+F32 = mybir.dt.float32
+BF16 = mybir.dt.bfloat16
+I32 = mybir.dt.int32
+U32 = mybir.dt.uint32
+U16 = mybir.dt.uint16
+U8 = mybir.dt.uint8
+FP8X4 = mybir.dt.float8_e4m3fn_x4
+ACT = mybir.ActivationFunctionType
+MULT = mybir.AluOpType.mult
+ADD = mybir.AluOpType.add
+
+LOADS = (
+    (0, 0, 256), (0, 256, 512), (0, 768, 768),
+    (1, 0, 768), (1, 768, 768),
+    (2, 0, 768), (2, 768, 512), (2, 1280, 256),
+)
+VECTOR_SHARE = (8, 9, 9, 2, 0, 0, 0, 8)
+
+
+def tile_moe_cap2_lin_relu2_kernel(tc, xT, w_words, w_scales, b, gate, offs, pos1, pos2, out):
+    nc = tc.nc
+    with ExitStack() as ctx:
+        keep = ctx.enter_context(tc.tile_pool(name="keep", bufs=1))
+        psum = ctx.enter_context(tc.psum_pool(name="psum", bufs=1))
+
+        offs_sb = keep.tile([P, S // 16], U16, name="offs_sb")
+        pos1_sb = keep.tile([P, T // 16], U16, name="pos1_sb")
+        pos2_sb = keep.tile([P, T // 16], U16, name="pos2_sb")
+        codes = [keep.tile([P, T], U32, name=f"codes{a}", align_bytes=64) for a in range(PASSES)]
+        planes = keep.tile([P, T], U8, name="planes", align_bytes=64)
+        slot_codes = [keep.tile([P, S], U32, name=f"slot_codes{a}", align_bytes=64) for a in range(PASSES)]
+        slot_planes = keep.tile([P, S], U8, name="slot_planes", align_bytes=64)
+        w_sb = keep.tile([P, E * PASSES, N], U32, name="w_sb", align_bytes=64)
+        w_planes = keep.tile([P, E * N], U8, name="w_planes", align_bytes=64)
+        b_sb = keep.tile([P, E], F32, name="b_sb")
+        gate_sb = [keep.tile([P, T], F32, name=f"gate_sb{g}") for g in range(2)]
+        y = keep.tile([P, S + PAD], F32, name="y")
+        warm = keep.tile([P, 8], F32, name="warm")
+        warmed = keep.tile([P, 8], F32, name="warmed")
+        banks = [psum.tile([P, C], F32, name=f"bank{e}") for e in range(E)]
+
+        nc.vector.memset(warm[:], 0.0)
+        nc.scalar.activation(warmed[:], warm[:], ACT.Square)
+        nc.vector.memset(w_planes[:].bitcast(I32), 0)
+        nc.vector.memset(planes[:].bitcast(I32), 0)
+
+        raws = []
+        for i, (a, t0, width) in enumerate(LOADS):
+            raw = keep.tile([P, PACK, width], F32, name=f"raw{i}")
+            nc.sync.dma_start(out=raw[:], in_=xT[a * K_PASS : (a + 1) * K_PASS, t0 : t0 + width].rearrange("(p j) t -> p j t", j=PACK))
+            raws.append(raw)
+            if i == 1:
+                nc.sync.dma_start(offs_sb[:], offs)
+        scale_rows = w_scales.rearrange("e a (q r) n -> a r q e n", r=4)
+        for a in range(PASSES):
+            for r in range(4):
+                nc.gpsimd.dma_start(
+                    out=w_planes[4 * a + r : P : 32, :].bitcast(I32).rearrange("q (e n) -> q e n", e=E),
+                    in_=scale_rows[a, r].bitcast(I32),
+                )
+        nc.gpsimd.dma_start(out=b_sb[:], in_=b)
+        nc.gpsimd.memset(y[:, S : S + PAD], 0.0)
+        for e in range(0, E, 2):
+            nc.sync.dma_start(
+                out=w_sb[:, e * PASSES : (e + 2) * PASSES, :].bitcast(I32),
+                in_=w_words[e : e + 2].rearrange("e a p n r -> p (e a) (n r)").bitcast(I32),
+            )
+        nc.sync.dma_start(pos1_sb[:], pos1)
+        nc.sync.dma_start(pos2_sb[:], pos2)
+        for g in range(2):
+            nc.sync.dma_start(out=gate_sb[g][:], in_=gate[g])
+
+        for i, (a, t0, width) in enumerate(LOADS):
+            for u0 in range(0, width, 512):
+                n = min(512, width - u0)
+                grouped = keep.tile([P, n, PACK], BF16, name=f"grouped{i}_{u0}", align_bytes=64)
+                cut = n - n * VECTOR_SHARE[i] // 16
+                for lo, hi, engine in ((0, cut, 0), (cut, n, 1)):
+                    if lo == hi:
+                        continue
+                    dst = grouped[:, lo:hi, :].rearrange("p (c i) j -> p c j i", i=4)
+                    source = raws[i][:, :, u0 + lo : u0 + hi].rearrange("p j (c i) -> p c j i", i=4)
+                    if engine == 0:
+                        nc.scalar.activation(dst, source, ACT.Copy)
+                    else:
+                        nc.vector.tensor_copy(dst, source)
+                cols = slice(t0 + u0, t0 + u0 + n)
+                nc.vector.quantize_mx(
+                    out=codes[a][:, cols].bitcast(FP8X4),
+                    scales=planes[4 * a : P, cols],
+                    in_=grouped[:].rearrange("p t j -> p (t j)"),
+                )
+
+        def gather(dst, window, lo, hi):
+            nc.vector.tensor_copy(dst[:, lo:hi], window[:].indirect(offs_sb[:, lo // 16 : hi // 16]))
+
+        for a in range(PASSES - 1):
+            for lo in range(0, S, 1024):
+                gather(slot_codes[a], codes[a], lo, lo + 1024)
+
+        for lo, hi in ((0, 512), (512, 1024), (1024, 1536), (1536, 1792), (1792, 2048)):
+            gather(slot_planes, planes, lo, hi)
+            gather(slot_codes[PASSES - 1], codes[PASSES - 1], lo, hi)
+            for e in range(lo // C, hi // C):
+                slots = slice(e * C, (e + 1) * C)
+                for a in range(PASSES):
+                    nc.tensor.matmul_mx(
+                        out=banks[e][:],
+                        lhsT=w_sb[:, e * PASSES + a, :].bitcast(FP8X4),
+                        lhsT_scale=w_planes[4 * a : P, e * N : (e + 1) * N],
+                        rhs=slot_codes[a][:, slots].bitcast(FP8X4),
+                        rhs_scale=slot_planes[4 * a : P, slots],
+                        start=(a == 0),
+                        stop=(a == PASSES - 1),
+                    )
+                relu = keep.tile([P, C], F32, name=f"relu{e}")
+                nc.scalar.activation(relu[:], banks[e][:], ACT.Relu, bias=b_sb[:, e : e + 1])
+                nc.scalar.activation(y[:, slots], relu[:], ACT.Square)
+
+        for i, (lo, hi) in enumerate(((0, 768), (768, 1280), (1280, 1536))):
+            picked = []
+            for g, pos_sb in enumerate((pos1_sb, pos2_sb)):
+                z = keep.tile([P, hi - lo], F32, name=f"z{g}_{i}")
+                nc.vector.tensor_tensor(z[:], y[:].indirect(pos_sb[:, lo // 16 : hi // 16]), gate_sb[g][:, lo:hi], MULT)
+                picked.append(z)
+            total = keep.tile([P, hi - lo], F32, name=f"total{i}")
+            nc.vector.tensor_tensor(total[:], picked[0][:], picked[1][:], ADD)
+            nc.sync.dma_start(out=out[:, lo:hi], in_=total[:])

@@ -24,11 +24,11 @@ MULT = mybir.AluOpType.mult
 ADD = mybir.AluOpType.add
 
 LOADS = (
-    (0, 0, 256), (0, 256, 512), (0, 768, 768),
-    (1, 0, 768), (1, 768, 768),
-    (2, 0, 768), (2, 768, 512), (2, 1280, 256),
+    (0, 0, 512), (0, 512, 512), (0, 1024, 512),
+    (1, 0, 512), (1, 512, 512), (1, 1024, 512),
+    (2, 0, 512), (2, 512, 512), (2, 1024, 256), (2, 1280, 256),
 )
-VECTOR_SHARE = (8, 9, 9, 2, 0, 0, 0, 8)
+VECTOR_SHARE = (4, 8, 8, 0, 0, 4, 0, 0, 0, 6)
 
 
 def tile_moe_cap2_lin_relu2_kernel(tc, xT, w_words, w_scales, b, gate, offs, pos1, pos2, out):
@@ -65,6 +65,7 @@ def tile_moe_cap2_lin_relu2_kernel(tc, xT, w_words, w_scales, b, gate, offs, pos
             raws.append(raw)
             if i == 1:
                 nc.sync.dma_start(offs_sb[:], offs)
+        nc.gpsimd.dma_start(out=b_sb[:], in_=b)
         scale_rows = w_scales.rearrange("e a (q r) n -> a r q e n", r=4)
         for a in range(PASSES):
             for r in range(4):
@@ -72,7 +73,6 @@ def tile_moe_cap2_lin_relu2_kernel(tc, xT, w_words, w_scales, b, gate, offs, pos
                     out=w_planes[4 * a + r : P : 32, :].bitcast(I32).rearrange("q (e n) -> q e n", e=E),
                     in_=scale_rows[a, r].bitcast(I32),
                 )
-        nc.gpsimd.dma_start(out=b_sb[:], in_=b)
         nc.gpsimd.memset(y[:, S : S + PAD], 0.0)
         for e in range(0, E, 2):
             nc.sync.dma_start(
@@ -81,14 +81,15 @@ def tile_moe_cap2_lin_relu2_kernel(tc, xT, w_words, w_scales, b, gate, offs, pos
             )
         nc.sync.dma_start(pos1_sb[:], pos1)
         nc.sync.dma_start(pos2_sb[:], pos2)
-        for g in range(2):
-            nc.sync.dma_start(out=gate_sb[g][:], in_=gate[g])
+        for half in (slice(0, 768), slice(768, T)):
+            for g in range(2):
+                nc.sync.dma_start(out=gate_sb[g][:, half], in_=gate[g, :, half])
 
         for i, (a, t0, width) in enumerate(LOADS):
             for u0 in range(0, width, 512):
                 n = min(512, width - u0)
                 grouped = keep.tile([P, n, PACK], BF16, name=f"grouped{i}_{u0}", align_bytes=64)
-                cut = n - n * VECTOR_SHARE[i] // 16
+                cut = n - n * VECTOR_SHARE[i] // 128 * 8
                 for lo, hi, engine in ((0, cut, 0), (cut, n, 1)):
                     if lo == hi:
                         continue

from contextlib import ExitStack

import concourse.mybir as mybir

K, T, E, C, N = 1536, 1536, 8, 256, 128
S = E * C
PAD = 32
P = 128
PACK = 4
K_PASS = P * PACK
PASSES = K // K_PASS

FLOPS = 2 * K * N * S

F32 = mybir.dt.float32
BF16 = mybir.dt.bfloat16
I32 = mybir.dt.int32
U32 = mybir.dt.uint32
U16 = mybir.dt.uint16
U8 = mybir.dt.uint8
FP8X4 = mybir.dt.float8_e4m3fn_x4
ACT = mybir.ActivationFunctionType
MULT = mybir.AluOpType.mult
ADD = mybir.AluOpType.add

LOADS = (
    (0, 0, 512), (0, 512, 512), (0, 1024, 512),
    (1, 0, 512), (1, 512, 512), (1, 1024, 512),
    (2, 0, 512), (2, 512, 512), (2, 1024, 256), (2, 1280, 256),
)
VECTOR_SHARE = (4, 8, 8, 0, 0, 4, 0, 0, 0, 6)


def tile_moe_cap2_lin_relu2_kernel(tc, xT, w_words, w_scales, b, gate, offs, pos1, pos2, out):
    nc = tc.nc
    with ExitStack() as ctx:
        keep = ctx.enter_context(tc.tile_pool(name="keep", bufs=1))
        psum = ctx.enter_context(tc.psum_pool(name="psum", bufs=1))

        offs_sb = keep.tile([P, S // 16], U16, name="offs_sb")
        pos1_sb = keep.tile([P, T // 16], U16, name="pos1_sb")
        pos2_sb = keep.tile([P, T // 16], U16, name="pos2_sb")
        codes = [keep.tile([P, T], U32, name=f"codes{a}", align_bytes=64) for a in range(PASSES)]
        planes = keep.tile([P, T], U8, name="planes", align_bytes=64)
        slot_codes = [keep.tile([P, S], U32, name=f"slot_codes{a}", align_bytes=64) for a in range(PASSES)]
        slot_planes = keep.tile([P, S], U8, name="slot_planes", align_bytes=64)
        w_sb = keep.tile([P, E * PASSES, N], U32, name="w_sb", align_bytes=64)
        w_planes = keep.tile([P, E * N], U8, name="w_planes", align_bytes=64)
        b_sb = keep.tile([P, E], F32, name="b_sb")
        gate_sb = [keep.tile([P, T], F32, name=f"gate_sb{g}") for g in range(2)]
        y = keep.tile([P, S + PAD], F32, name="y")
        warm = keep.tile([P, 8], F32, name="warm")
        warmed = keep.tile([P, 8], F32, name="warmed")
        banks = [psum.tile([P, C], F32, name=f"bank{e}") for e in range(E)]

        nc.vector.memset(warm[:], 0.0)
        nc.scalar.activation(warmed[:], warm[:], ACT.Square)
        nc.vector.memset(w_planes[:].bitcast(I32), 0)
        nc.vector.memset(planes[:].bitcast(I32), 0)

        raws = []
        for i, (a, t0, width) in enumerate(LOADS):
            raw = keep.tile([P, PACK, width], F32, name=f"raw{i}")
            nc.sync.dma_start(out=raw[:], in_=xT[a * K_PASS : (a + 1) * K_PASS, t0 : t0 + width].rearrange("(p j) t -> p j t", j=PACK))
            raws.append(raw)
            if i == 1:
                nc.sync.dma_start(offs_sb[:], offs)
        nc.gpsimd.dma_start(out=b_sb[:], in_=b)
        scale_rows = w_scales.rearrange("e a (q r) n -> a r q e n", r=4)
        for a in range(PASSES):
            for r in range(4):
                nc.gpsimd.dma_start(
                    out=w_planes[4 * a + r : P : 32, :].bitcast(I32).rearrange("q (e n) -> q e n", e=E),
                    in_=scale_rows[a, r].bitcast(I32),
                )
        nc.gpsimd.memset(y[:, S : S + PAD], 0.0)
        for e in range(0, E, 2):
            nc.sync.dma_start(
                out=w_sb[:, e * PASSES : (e + 2) * PASSES, :].bitcast(I32),
                in_=w_words[e : e + 2].rearrange("e a p n r -> p (e a) (n r)").bitcast(I32),
            )
        nc.sync.dma_start(pos1_sb[:], pos1)
        nc.sync.dma_start(pos2_sb[:], pos2)
        for half in (slice(0, 768), slice(768, T)):
            for g in range(2):
                nc.sync.dma_start(out=gate_sb[g][:, half], in_=gate[g, :, half])

        for i, (a, t0, width) in enumerate(LOADS):
            for u0 in range(0, width, 512):
                n = min(512, width - u0)
                grouped = keep.tile([P, n, PACK], BF16, name=f"grouped{i}_{u0}", align_bytes=64)
                cut = n - n * VECTOR_SHARE[i] // 128 * 8
                for lo, hi, engine in ((0, cut, 0), (cut, n, 1)):
                    if lo == hi:
                        continue
                    dst = grouped[:, lo:hi, :].rearrange("p (c i) j -> p c j i", i=4)
                    source = raws[i][:, :, u0 + lo : u0 + hi].rearrange("p j (c i) -> p c j i", i=4)
                    if engine == 0:
                        nc.scalar.activation(dst, source, ACT.Copy)
                    else:
                        nc.vector.tensor_copy(dst, source)
                cols = slice(t0 + u0, t0 + u0 + n)
                nc.vector.quantize_mx(
                    out=codes[a][:, cols].bitcast(FP8X4),
                    scales=planes[4 * a : P, cols],
                    in_=grouped[:].rearrange("p t j -> p (t j)"),
                )

        def gather(dst, window, lo, hi):
            nc.vector.tensor_copy(dst[:, lo:hi], window[:].indirect(offs_sb[:, lo // 16 : hi // 16]))

        for a in range(PASSES - 1):
            for lo in range(0, S, 1024):
                gather(slot_codes[a], codes[a], lo, lo + 1024)

        for lo, hi in ((0, 512), (512, 1024), (1024, 1536), (1536, 1792), (1792, 2048)):
            gather(slot_planes, planes, lo, hi)
            gather(slot_codes[PASSES - 1], codes[PASSES - 1], lo, hi)
            for e in range(lo // C, hi // C):
                slots = slice(e * C, (e + 1) * C)
                for a in range(PASSES):
                    nc.tensor.matmul_mx(
                        out=banks[e][:],
                        lhsT=w_sb[:, e * PASSES + a, :].bitcast(FP8X4),
                        lhsT_scale=w_planes[4 * a : P, e * N : (e + 1) * N],
                        rhs=slot_codes[a][:, slots].bitcast(FP8X4),
                        rhs_scale=slot_planes[4 * a : P, slots],
                        start=(a == 0),
                        stop=(a == PASSES - 1),
                    )
                relu = keep.tile([P, C], F32, name=f"relu{e}")
                nc.scalar.activation(relu[:], banks[e][:], ACT.Relu, bias=b_sb[:, e : e + 1])
                nc.scalar.activation(y[:, slots], relu[:], ACT.Square)

        for i, (lo, hi) in enumerate(((0, 768), (768, 1280), (1280, 1536))):
            picked = []
            for g, pos_sb in enumerate((pos1_sb, pos2_sb)):
                z = keep.tile([P, hi - lo], F32, name=f"z{g}_{i}")
                nc.vector.tensor_tensor(z[:], y[:].indirect(pos_sb[:, lo // 16 : hi // 16]), gate_sb[g][:, lo:hi], MULT)
                picked.append(z)
            total = keep.tile([P, hi - lo], F32, name=f"total{i}")
            nc.vector.tensor_tensor(total[:], picked[0][:], picked[1][:], ADD)
            nc.sync.dma_start(out=out[:, lo:hi], in_=total[:])
